import numpy as np
import ml_dtypes

BF16 = ml_dtypes.bfloat16


def bf(x):
    return np.asarray(x, np.float32).astype(BF16)


def f32(x):
    return np.asarray(x, np.float32)


def f64(x):
    return np.asarray(x).astype(np.float64)


def striped(idx):
    return np.tile(idx.reshape(-1, 16).T, (8, 1))


S, K, M, N, D = 1024, 256, 128, 128, 256


def setup_inputs():
    return {"table": bf(np.random.standard_normal((K, S))), "qry": bf(1.5 * np.random.standard_normal((K, M)) / np.sqrt(K)), "w": bf(np.random.standard_normal((K, D)) / np.sqrt(K)), "r": f32(0.7 * np.random.standard_normal((1, N))), "offs": striped(np.random.permutation(S)[:N])}


def reference(table, qry, w, r, offs):
    idx = offs[:16].T.reshape(-1)
    x = f64(table)[:, idx]
    a = f64(qry).T @ x + f64(r)
    a = np.exp(a - a.max(axis=1, keepdims=True))
    a = a / a.sum(axis=1, keepdims=True)
    return a @ (f64(w).T @ x).T

@@ -1,0 +1,77 @@
+import concourse.mybir as mybir
+from concourse.masks import make_identity
+
+P = 128
+BF16, F32, U16 = mybir.dt.bfloat16, mybir.dt.float32, mybir.dt.uint16
+EXP, COPY = mybir.ActivationFunctionType.Exp, mybir.ActivationFunctionType.Copy
+
+FLOPS = 2 * 256 * 128 * 128 + 2 * 256 * 256 * 128 + 2 * 128 * 128 * 256
+
+
+def tile_rows_dsa_sub_kernel(tc, table, qry, w, r, offs, out):
+    nc = tc.nc
+    n_features, n_positions = table.shape
+    n_queries, n_picked, n_values = qry.shape[1], r.shape[1], w.shape[1]
+    halves, value_blocks = n_features // P, n_values // P
+
+    with tc.tile_pool(name="sbuf", bufs=1) as sbuf, tc.psum_pool(name="psum", bufs=1) as psum:
+        offsets = sbuf.tile([P, n_picked // 16], U16, name="offsets")
+        nc.sync.dma_start(offsets[:], offs)
+        table_halves = table.rearrange("(p h) s -> h p s", h=halves)
+        latents = [sbuf.tile([P, n_positions], BF16, name=f"latents{h}") for h in range(halves)]
+        for h in range(halves):
+            nc.sync.dma_start(latents[h][:], table_halves[h])
+        bias = sbuf.tile([1, n_picked], F32, name="bias")
+        nc.scalar.dma_start(bias[:], r)
+        queries = sbuf.tile([P, halves, n_queries], BF16, name="queries")
+        nc.scalar.dma_start(queries[:], qry.rearrange("(p h) m -> p h m", h=halves))
+        weights = sbuf.tile([P, halves, n_values], BF16, name="weights")
+        nc.scalar.dma_start(weights[:], w.rearrange("(p h) d -> p h d", h=halves))
+
+        identity = sbuf.tile([P, P], BF16, name="identity")
+        make_identity(nc, identity[:])
+        ones = sbuf.tile([1, n_queries], F32, name="ones")
+        nc.vector.memset(ones[:], 1.0)
+
+        scores = psum.tile([n_queries, n_picked], F32, name="scores")
+        nc.tensor.matmul(scores[:], ones[:], bias[:], start=True, stop=False)
+
+        values = [psum.tile([P, n_picked], F32, name=f"values{b}") for b in range(value_blocks)]
+        for h in range(halves):
+            picked = latents[h][:].indirect(offsets[:])
+            last = h == halves - 1
+            nc.tensor.matmul(scores[:], queries[:, h, :], picked, start=False, stop=last)
+            for b in range(value_blocks):
+                nc.tensor.matmul(values[b][:], weights[:, h, b * P : (b + 1) * P], picked, start=h == 0, stop=last)
+
+        minus_max = sbuf.tile([n_queries, 1], F32, name="minus_max")
+        nc.vector.reduce_max(minus_max[:], scores[:], mybir.AxisListType.X, negate=True)
+        exps = sbuf.tile([n_queries, n_picked], BF16, name="exps")
+        row_sum = sbuf.tile([n_queries, 1], F32, name="row_sum")
+        nc.scalar.activation(exps[:], scores[:], EXP, bias=minus_max[:], accum_out=row_sum[:])
+        inverse_sum = sbuf.tile([n_queries, 1], F32, name="inverse_sum")
+        nc.vector.reciprocal(inverse_sum[:], row_sum[:])
+
+        exps_t_psum = psum.tile([n_picked, n_queries], BF16, name="exps_t_psum")
+        nc.tensor.transpose(exps_t_psum[:], exps[:], identity[:])
+        exps_t = sbuf.tile([n_picked, n_queries], BF16, name="exps_t")
+        nc.scalar.copy(exps_t[:], exps_t_psum[:])
+
+        for b in range(value_blocks):
+            rounded = sbuf.tile([P, n_picked], BF16, name=f"rounded{b}")
+            nc.vector.tensor_copy(rounded[:], values[b][:])
+            values_t_psum = psum.tile([n_picked, P], BF16, name=f"values_t_psum{b}")
+            nc.tensor.transpose(values_t_psum[:], rounded[:], identity[:])
+            values_t = sbuf.tile([n_picked, P], BF16, name=f"values_t{b}")
+            nc.vector.tensor_copy(values_t[:], values_t_psum[:])
+
+            mixed = psum.tile([n_queries, P], F32, name=f"mixed{b}")
+            nc.tensor.matmul(mixed[:], exps_t[:], values_t[:], start=True, stop=True)
+
+            result = sbuf.tile([n_queries, P], F32, name=f"result{b}")
+            if b % 2 == 0:
+                nc.vector.tensor_scalar_mul(result[:], mixed[:], inverse_sum[:])
+                nc.sync.dma_start(out[:, b * P : (b + 1) * P], result[:])
+            else:
+                nc.scalar.activation(result[:], mixed[:], COPY, scale=inverse_sum[:])
+                nc.scalar.dma_start(out[:, b * P : (b + 1) * P], result[:])

@@ -57,6 +57,7 @@ def tile_rows_dsa_sub_kernel(tc, table, qry, w, r, offs, out):
         exps_t = sbuf.tile([n_picked, n_queries], BF16, name="exps_t")
         nc.scalar.copy(exps_t[:], exps_t_psum[:])
 
+        result = sbuf.tile([n_queries, n_values], F32, name="result")
         for b in range(value_blocks):
             rounded = sbuf.tile([P, n_picked], BF16, name=f"rounded{b}")
             nc.vector.tensor_copy(rounded[:], values[b][:])
@@ -68,10 +69,10 @@ def tile_rows_dsa_sub_kernel(tc, table, qry, w, r, offs, out):
             mixed = psum.tile([n_queries, P], F32, name=f"mixed{b}")
             nc.tensor.matmul(mixed[:], exps_t[:], values_t[:], start=True, stop=True)
 
-            result = sbuf.tile([n_queries, P], F32, name=f"result{b}")
+            columns = result[:, b * P : (b + 1) * P]
             if b % 2 == 0:
-                nc.vector.tensor_scalar_mul(result[:], mixed[:], inverse_sum[:])
-                nc.sync.dma_start(out[:, b * P : (b + 1) * P], result[:])
+                nc.vector.tensor_scalar_mul(columns, mixed[:], inverse_sum[:])
             else:
-                nc.scalar.activation(result[:], mixed[:], COPY, scale=inverse_sum[:])
-                nc.scalar.dma_start(out[:, b * P : (b + 1) * P], result[:])
+                nc.scalar.activation(columns, mixed[:], COPY, scale=inverse_sum[:])
+
+        nc.sync.dma_start(out, result[:])

@@ -3,7 +3,7 @@ from concourse.masks import make_identity
 
 P = 128
 BF16, F32, U16 = mybir.dt.bfloat16, mybir.dt.float32, mybir.dt.uint16
-EXP, COPY = mybir.ActivationFunctionType.Exp, mybir.ActivationFunctionType.Copy
+EXP = mybir.ActivationFunctionType.Exp
 
 FLOPS = 2 * 256 * 128 * 128 + 2 * 256 * 256 * 128 + 2 * 128 * 128 * 256
 
@@ -17,16 +17,14 @@ def tile_rows_dsa_sub_kernel(tc, table, qry, w, r, offs, out):
     with tc.tile_pool(name="sbuf", bufs=1) as sbuf, tc.psum_pool(name="psum", bufs=1) as psum:
         offsets = sbuf.tile([P, n_picked // 16], U16, name="offsets")
         nc.sync.dma_start(offsets[:], offs)
-        table_halves = table.rearrange("(p h) s -> h p s", h=halves)
-        latents = [sbuf.tile([P, n_positions], BF16, name=f"latents{h}") for h in range(halves)]
-        for h in range(halves):
-            nc.sync.dma_start(latents[h][:], table_halves[h])
+        latents = sbuf.tile([P, halves, n_positions], BF16, name="latents")
+        nc.sync.dma_start(latents[:], table.rearrange("(p h) s -> p h s", h=halves))
+        weights = sbuf.tile([P, halves, n_values], BF16, name="weights")
+        nc.sync.dma_start(weights[:], w.rearrange("(p h) d -> p h d", h=halves))
         bias = sbuf.tile([1, n_picked], F32, name="bias")
         nc.scalar.dma_start(bias[:], r)
         queries = sbuf.tile([P, halves, n_queries], BF16, name="queries")
         nc.scalar.dma_start(queries[:], qry.rearrange("(p h) m -> p h m", h=halves))
-        weights = sbuf.tile([P, halves, n_values], BF16, name="weights")
-        nc.scalar.dma_start(weights[:], w.rearrange("(p h) d -> p h d", h=halves))
 
         identity = sbuf.tile([P, P], BF16, name="identity")
         make_identity(nc, identity[:])
@@ -37,12 +35,13 @@ def tile_rows_dsa_sub_kernel(tc, table, qry, w, r, offs, out):
         nc.tensor.matmul(scores[:], ones[:], bias[:], start=True, stop=False)
 
         values = [psum.tile([P, n_picked], F32, name=f"values{b}") for b in range(value_blocks)]
+        picked = [latents[:, h, :].indirect(offsets[:]) for h in range(halves)]
         for h in range(halves):
-            picked = latents[h][:].indirect(offsets[:])
-            last = h == halves - 1
-            nc.tensor.matmul(scores[:], queries[:, h, :], picked, start=False, stop=last)
-            for b in range(value_blocks):
-                nc.tensor.matmul(values[b][:], weights[:, h, b * P : (b + 1) * P], picked, start=h == 0, stop=last)
+            nc.tensor.matmul(scores[:], queries[:, h, :], picked[h], start=False, stop=h == halves - 1)
+        for b in range(value_blocks):
+            for h in range(halves):
+                block = weights[:, h, b * P : (b + 1) * P]
+                nc.tensor.matmul(values[b][:], block, picked[h], start=h == 0, stop=h == halves - 1)
 
         minus_max = sbuf.tile([n_queries, 1], F32, name="minus_max")
         nc.vector.reduce_max(minus_max[:], scores[:], mybir.AxisListType.X, negate=True)
@@ -70,9 +69,6 @@ def tile_rows_dsa_sub_kernel(tc, table, qry, w, r, offs, out):
             nc.tensor.matmul(mixed[:], exps_t[:], values_t[:], start=True, stop=True)
 
             columns = result[:, b * P : (b + 1) * P]
-            if b % 2 == 0:
-                nc.vector.tensor_scalar_mul(columns, mixed[:], inverse_sum[:])
-            else:
-                nc.scalar.activation(columns, mixed[:], COPY, scale=inverse_sum[:])
+            nc.vector.tensor_scalar_mul(columns, mixed[:], inverse_sum[:])
 
         nc.sync.dma_start(out, result[:])

import concourse.mybir as mybir
from concourse.masks import make_identity

P = 128
BF16, F32, U16 = mybir.dt.bfloat16, mybir.dt.float32, mybir.dt.uint16
EXP = mybir.ActivationFunctionType.Exp

FLOPS = 2 * 256 * 128 * 128 + 2 * 256 * 256 * 128 + 2 * 128 * 128 * 256


def tile_rows_dsa_sub_kernel(tc, table, qry, w, r, offs, out):
    nc = tc.nc
    n_features, n_positions = table.shape
    n_queries, n_picked, n_values = qry.shape[1], r.shape[1], w.shape[1]
    halves, value_blocks = n_features // P, n_values // P

    with tc.tile_pool(name="sbuf", bufs=1) as sbuf, tc.psum_pool(name="psum", bufs=1) as psum:
        offsets = sbuf.tile([P, n_picked // 16], U16, name="offsets")
        nc.sync.dma_start(offsets[:], offs)
        latents = sbuf.tile([P, halves, n_positions], BF16, name="latents")
        nc.sync.dma_start(latents[:], table.rearrange("(p h) s -> p h s", h=halves))
        weights = sbuf.tile([P, halves, n_values], BF16, name="weights")
        nc.sync.dma_start(weights[:], w.rearrange("(p h) d -> p h d", h=halves))
        bias = sbuf.tile([1, n_picked], F32, name="bias")
        nc.scalar.dma_start(bias[:], r)
        queries = sbuf.tile([P, halves, n_queries], BF16, name="queries")
        nc.scalar.dma_start(queries[:], qry.rearrange("(p h) m -> p h m", h=halves))

        identity = sbuf.tile([P, P], BF16, name="identity")
        make_identity(nc, identity[:])
        ones = sbuf.tile([1, n_queries], F32, name="ones")
        nc.vector.memset(ones[:], 1.0)

        scores = psum.tile([n_queries, n_picked], F32, name="scores")
        nc.tensor.matmul(scores[:], ones[:], bias[:], start=True, stop=False)

        values = [psum.tile([P, n_picked], F32, name=f"values{b}") for b in range(value_blocks)]
        picked = [latents[:, h, :].indirect(offsets[:]) for h in range(halves)]
        for h in range(halves):
            nc.tensor.matmul(scores[:], queries[:, h, :], picked[h], start=False, stop=h == halves - 1)
        for b in range(value_blocks):
            for h in range(halves):
                block = weights[:, h, b * P : (b + 1) * P]
                nc.tensor.matmul(values[b][:], block, picked[h], start=h == 0, stop=h == halves - 1)

        minus_max = sbuf.tile([n_queries, 1], F32, name="minus_max")
        nc.vector.reduce_max(minus_max[:], scores[:], mybir.AxisListType.X, negate=True)
        exps = sbuf.tile([n_queries, n_picked], BF16, name="exps")
        row_sum = sbuf.tile([n_queries, 1], F32, name="row_sum")
        nc.scalar.activation(exps[:], scores[:], EXP, bias=minus_max[:], accum_out=row_sum[:])
        inverse_sum = sbuf.tile([n_queries, 1], F32, name="inverse_sum")
        nc.vector.reciprocal(inverse_sum[:], row_sum[:])

        exps_t_psum = psum.tile([n_picked, n_queries], BF16, name="exps_t_psum")
        nc.tensor.transpose(exps_t_psum[:], exps[:], identity[:])
        exps_t = sbuf.tile([n_picked, n_queries], BF16, name="exps_t")
        nc.scalar.copy(exps_t[:], exps_t_psum[:])

        result = sbuf.tile([n_queries, n_values], F32, name="result")
        for b in range(value_blocks):
            rounded = sbuf.tile([P, n_picked], BF16, name=f"rounded{b}")
            nc.vector.tensor_copy(rounded[:], values[b][:])
            values_t_psum = psum.tile([n_picked, P], BF16, name=f"values_t_psum{b}")
            nc.tensor.transpose(values_t_psum[:], rounded[:], identity[:])
            values_t = sbuf.tile([n_picked, P], BF16, name=f"values_t{b}")
            nc.vector.tensor_copy(values_t[:], values_t_psum[:])

            mixed = psum.tile([n_queries, P], F32, name=f"mixed{b}")
            nc.tensor.matmul(mixed[:], exps_t[:], values_t[:], start=True, stop=True)

            columns = result[:, b * P : (b + 1) * P]
            nc.vector.tensor_scalar_mul(columns, mixed[:], inverse_sum[:])

        nc.sync.dma_start(out, result[:])
